import numpy as np, ml_dtypes
CORES = [21,85,149,213,277,341,405,469]
N = 8
import mx_ref
NC, G, D = 128, 2, 64
C = np.float32(0.023)
BF = ml_dtypes.bfloat16
def cut(t, i, w=512):
    return t[:, w * i:w * i + w]
def tile(rs):
    return np.stack(rs, axis=2).reshape(128, -1).astype(BF)
def layer(w, X):
    out = []
    for i in range(G):
        for t in range(len(X)):
            p = mx_ref.matmul(mx_ref.quantize(cut(w, len(X) * i + t)), X[t])
            z = p if t == 0 else z + p
        out.append(z)
    return out
def act(Z):
    return [np.maximum(s * z, 0) * C for z in Z for s in (1, -1)]
def setup_inputs(rng):
    def f(*shape):
        return mx_ref.flush((rng.standard_normal(shape, dtype=np.float32) * np.exp2(rng.integers(-2, 3, shape[:-1] + (1,)))).astype(BF))
    return {"x": f(N, 128, 4 * NC), "w1": f(N, 128, G * 512), "wt": f(N, 128, 3 * 512)}
def setup_inputs_blocks(rng):
    d = setup_inputs(rng)
    for k in ("x", "wt", "w1"): d[k] = mx_ref.spread(d[k], rng, 2)
    return d
def setup_inputs_wide(rng):
    d = setup_inputs(rng)
    for k in ("wt",): d[k] = mx_ref.flush((d[k].astype(np.float32) * np.exp2(rng.integers(-6, 7, (N, 1, 1))).astype(np.float32)).astype(BF))
    return d
def setup_inputs_zeros(rng):
    d = setup_inputs(rng); v = d["x"].reshape(N, 128, -1, 4).copy()
    v[np.broadcast_to((rng.random((N, 1, v.shape[2], 1)) < 0.33), v.shape)] = 0
    d["x"] = v.reshape(d["x"].shape)
    return d
def reference(x, w1, wt):
    h = [tile(act(layer(w1[j], [mx_ref.quantize(x[j])]))) for j in range(N)]
    y = np.zeros((N, 128, NC), np.float32)
    for r in range(N):
        e = np.concatenate([h[(r - 1) % N][:, 4 * (NC - D):], h[r], h[(r + 1) % N][:, :4 * D]], axis=1)
        for t in range(3):
            p = mx_ref.matmul(mx_ref.quantize(cut(wt[r], t)), mx_ref.quantize(e[:, 4 * D * t:4 * D * t + 4 * NC]))
            y[r] = p if t == 0 else y[r] + p
    return {"y": y}

@@ -1,0 +1,107 @@
+from concourse.bass import DstId, RemoteDMATransfer
+from concourse.mybir import dt, AluOpType, ActivationFunctionType
+
+NC, D = 128, 64
+C = 0.023
+NE = NC + 2 * D
+
+SCRATCH = {
+    "xs": ("sbuf", [128, 4 * NC], "bfloat16"),
+    "w1s": ("sbuf", [128, 2 * 512], "bfloat16"),
+    "wts": ("sbuf", [128, 3 * 512], "bfloat16"),
+    "h": ("sbuf", [128, 4 * NC], "bfloat16"),
+    "qx": ("sbuf", [128, NC], "float8_e4m3fn_x4"),
+    "sx": ("sbuf", [128, NC], "uint8"),
+    "qw": ("sbuf", [128, 2 * 128], "float8_e4m3fn_x4"),
+    "sw": ("sbuf", [128, 2 * 128], "uint8"),
+    "qt": ("sbuf", [128, 3 * 128], "float8_e4m3fn_x4"),
+    "st": ("sbuf", [128, 3 * 128], "uint8"),
+    "E": ("sbuf", [128, NE], "float8_e4m3fn_x4"),
+    "ES": ("sbuf", [128, NE], "uint8"),
+    "ys": ("sbuf", [128, NC], "float32"),
+    "z0": ("psum", [128, 512], "float32"),
+    "z1": ("psum", [128, 512], "float32"),
+    "yp": ("psum", [128, 512], "float32"),
+}
+SEMAPHORES = ["ldx", "ldw", "ldt", "q0", "q1", "m0", "m1", "hr", "hq", "tq", "ysum", "ycp", "stored",
+              "from_prev", "from_next", "sent"]
+
+
+def engines(mask):
+    return [1 << i for i in range(mask.bit_length()) if mask >> i & 1]
+
+
+def rank_program(g, core, T, topo):
+    r = T.rank_of(core)
+    if r is None:
+        return
+    n = len(T.cores)
+    prev, nxt = T.cores[(r - 1) % n], T.cores[(r + 1) % n]
+    S = T.sem
+
+    g.sync.dma_start(T.xs[:], T.x[:]).then_inc(S.ldx, 16)
+    g.scalar.dma_start(T.w1s[:], T.w1[:]).then_inc(S.ldw, 16)
+    g.sync.wait_ge(S.ldx, 16)
+    g.sync.dma_start(T.wts[:], T.wt[:]).then_inc(S.ldt, 16)
+
+    g.vector.wait_ge(S.ldx, 16)
+    g.vector.quantize_mx(T.qx[:], T.sx[:], T.xs[:]).then_inc(S.q0, 1)
+    g.vector.wait_ge(S.ldw, 16)
+    g.vector.quantize_mx(T.qw[:, 0:128], T.sw[:, 0:128], T.w1s[:, 0:512]).then_inc(S.q0, 1)
+    g.vector.quantize_mx(T.qw[:, 128:256], T.sw[:, 128:256], T.w1s[:, 512:1024]).then_inc(S.q1, 1)
+
+    g.tensor.wait_ge(S.q0, 2)
+    g.tensor.matmul_mx(T.z0[:, 0:NC], T.qw[:, 0:128], T.sw[:, 0:128], T.qx[:], T.sx[:], True, True).then_inc(S.m0, 1)
+    g.tensor.wait_ge(S.q1, 1)
+    g.tensor.matmul_mx(T.z1[:, 0:NC], T.qw[:, 128:256], T.sw[:, 128:256], T.qx[:], T.sx[:], True, True).then_inc(S.m1, 1)
+
+    relu = ActivationFunctionType.Relu
+    g.scalar.wait_ge(S.m0, 1)
+    g.scalar.activation(T.h[:, 0:4 * NC:4], T.z0[:, 0:NC], relu, scale=C).then_inc(S.hr, 1)
+    g.scalar.activation(T.h[:, 1:4 * NC:4], T.z0[:, 0:NC], relu, scale=-C).then_inc(S.hr, 1)
+    g.vector.wait_ge(S.m1, 1)
+    g.vector.tensor_scalar(T.h[:, 2:4 * NC:4], T.z1[:, 0:NC], 0.0, C, AluOpType.max, AluOpType.mult).then_inc(S.hr, 1)
+    g.vector.tensor_scalar(T.h[:, 3:4 * NC:4], T.z1[:, 0:NC], 0.0, -C, AluOpType.min, AluOpType.mult).then_inc(S.hr, 1)
+    g.vector.wait_ge(S.hr, 4)
+    g.vector.quantize_mx(T.E[:, D:D + NC], T.ES[:, D:D + NC], T.h[:]).then_inc(S.hq, 1)
+
+    es = engines(topo.mask(core, prev) & topo.mask(core, nxt))
+    halves = (es[0::2], es[1::2])
+
+    def halo(buf, cast):
+        out = []
+        for k, (dst, a, b, sem) in enumerate(((prev, D, D + NC, S.from_next), (nxt, NC, 0, S.from_prev))):
+            rid, pid = topo.addr(dst, core)
+            src, to = buf[:, a:a + D], buf[:, b:b + D]
+            if cast:
+                src, to = src.bitcast(dt.uint8), to.bitcast(dt.uint8)
+            out.append(RemoteDMATransfer(dst_ids=[DstId(rid=rid, pnc=pid)], dma_engine_mask=sum(halves[k]),
+                                         remote_sem=sem, src=src, dst=to))
+        return out
+
+    g.wait_ge(S.hq, 1)
+    g.remote_dma_fused(halo(T.E, True), local_sem=S.sent)
+    g.remote_dma_fused(halo(T.ES, False), local_sem=S.sent)
+    g.wait_ge(S.sent, 2 * len(es))
+
+    g.vector.wait_ge(S.ldt, 16)
+    g.vector.quantize_mx(T.qt[:], T.st[:], T.wts[:]).then_inc(S.tq, 1)
+
+    def tap(t, start, stop):
+        g.tensor.matmul_mx(T.yp[:, 0:NC], T.qt[:, 128 * t:128 * t + 128], T.st[:, 128 * t:128 * t + 128],
+                           T.E[:, D * t:D * t + NC], T.ES[:, D * t:D * t + NC], start, stop).then_inc(S.ysum, 1)
+
+    g.tensor.wait_ge(S.hq, 1)
+    g.tensor.wait_ge(S.tq, 1)
+    tap(1, True, False)
+    ends = [(0, prev, S.from_prev, len(halves[1])), (2, nxt, S.from_next, len(halves[0]))]
+    ends.sort(key=lambda e: topo.rack(topo.host(e[1])) != topo.rack(topo.host(core)))
+    for i, (t, _src, sem, cnt) in enumerate(ends):
+        g.tensor.wait_ge(sem, 2 * cnt)
+        tap(t, False, i == 1)
+
+    g.vector.wait_ge(S.ysum, 3)
+    g.vector.tensor_copy(T.ys[:], T.yp[:, 0:NC]).then_inc(S.ycp, 1)
+    g.sync.wait_ge(S.ycp, 1)
+    g.sync.dma_start(T.y[:], T.ys[:]).then_inc(S.stored, 16)
+    g.sync.wait_ge(S.stored, 16)

@@ -9,13 +9,15 @@ SCRATCH = {
     "xs": ("sbuf", [128, 4 * NC], "bfloat16"),
     "w1s": ("sbuf", [128, 2 * 512], "bfloat16"),
     "wts": ("sbuf", [128, 3 * 512], "bfloat16"),
-    "h": ("sbuf", [128, 4 * NC], "bfloat16"),
+    "h": ("sbuf", [128, 4 * (NC + D)], "bfloat16"),
     "qx": ("sbuf", [128, NC], "float8_e4m3fn_x4"),
     "sx": ("sbuf", [128, NC], "uint8"),
     "qw": ("sbuf", [128, 2 * 128], "float8_e4m3fn_x4"),
     "sw": ("sbuf", [128, 2 * 128], "uint8"),
     "qt": ("sbuf", [128, 3 * 128], "float8_e4m3fn_x4"),
     "st": ("sbuf", [128, 3 * 128], "uint8"),
+    "QF": ("sbuf", [128, NC], "float8_e4m3fn_x4"),
+    "SF": ("sbuf", [128, NC], "uint8"),
     "E": ("sbuf", [128, NE], "float8_e4m3fn_x4"),
     "ES": ("sbuf", [128, NE], "uint8"),
     "ys": ("sbuf", [128, NC], "float32"),
@@ -23,8 +25,8 @@ SCRATCH = {
     "z1": ("psum", [128, 512], "float32"),
     "yp": ("psum", [128, 512], "float32"),
 }
-SEMAPHORES = ["ldx", "ldw", "ldt", "q0", "q1", "m0", "m1", "hr", "hq", "tq", "ysum", "ycp", "stored",
-              "from_prev", "from_next", "sent"]
+SEMAPHORES = ["ldx", "ldw0", "ldw1", "ldt", "zero", "q0", "q1", "m0", "m1", "h1", "h2", "hf", "hq", "tq", "ysum", "ycp",
+              "stored", "from_prev", "from_next", "sent"]
 
 
 def engines(mask):
@@ -39,15 +41,26 @@ def rank_program(g, core, T, topo):
     prev, nxt = T.cores[(r - 1) % n], T.cores[(r + 1) % n]
     S = T.sem
 
+    first_is_next = topo.host(nxt) != topo.host(core)
+    z_first, z_second = (D, 0) if first_is_next else (0, D)
+    h_first, h_second, h_zero = (D, 0, NC) if first_is_next else (D, NC, 0)
+    pack = min(h_first, h_zero)
+    whole = min(h_first, h_second)
+    qf = h_first - pack
+
     g.sync.dma_start(T.xs[:], T.x[:]).then_inc(S.ldx, 16)
-    g.scalar.dma_start(T.w1s[:], T.w1[:]).then_inc(S.ldw, 16)
-    g.sync.wait_ge(S.ldx, 16)
+    g.scalar.dma_start(T.w1s[:, 0:512], T.w1[:, 0:512]).then_inc(S.ldw0, 16)
+    g.sync.dma_start(T.w1s[:, 512:1024], T.w1[:, 512:1024]).then_inc(S.ldw1, 16)
+    g.sync.wait_ge(S.ldw0, 16)
     g.sync.dma_start(T.wts[:], T.wt[:]).then_inc(S.ldt, 16)
 
+    g.vector.memset(T.h[:, 4 * h_zero:4 * (h_zero + D)], 0.0).then_inc(S.zero, 1)
+    g.vector.wait_ge(S.zero, 1)
     g.vector.wait_ge(S.ldx, 16)
     g.vector.quantize_mx(T.qx[:], T.sx[:], T.xs[:]).then_inc(S.q0, 1)
-    g.vector.wait_ge(S.ldw, 16)
+    g.vector.wait_ge(S.ldw0, 16)
     g.vector.quantize_mx(T.qw[:, 0:128], T.sw[:, 0:128], T.w1s[:, 0:512]).then_inc(S.q0, 1)
+    g.vector.wait_ge(S.ldw1, 16)
     g.vector.quantize_mx(T.qw[:, 128:256], T.sw[:, 128:256], T.w1s[:, 512:1024]).then_inc(S.q1, 1)
 
     g.tensor.wait_ge(S.q0, 2)
@@ -56,32 +69,45 @@ def rank_program(g, core, T, topo):
     g.tensor.matmul_mx(T.z1[:, 0:NC], T.qw[:, 128:256], T.sw[:, 128:256], T.qx[:], T.sx[:], True, True).then_inc(S.m1, 1)
 
     relu = ActivationFunctionType.Relu
+
+    def rows(b, at):
+        return T.h[:, 4 * at + b:4 * (at + D):4]
+
     g.scalar.wait_ge(S.m0, 1)
-    g.scalar.activation(T.h[:, 0:4 * NC:4], T.z0[:, 0:NC], relu, scale=C).then_inc(S.hr, 1)
-    g.scalar.activation(T.h[:, 1:4 * NC:4], T.z0[:, 0:NC], relu, scale=-C).then_inc(S.hr, 1)
+    for at, z, sem in ((h_first, z_first, S.h1), (h_second, z_second, S.h2)):
+        g.scalar.activation(rows(0, at), T.z0[:, z:z + D], relu, scale=C).then_inc(sem, 1)
+        g.scalar.activation(rows(1, at), T.z0[:, z:z + D], relu, scale=-C).then_inc(sem, 1)
     g.vector.wait_ge(S.m1, 1)
-    g.vector.tensor_scalar(T.h[:, 2:4 * NC:4], T.z1[:, 0:NC], 0.0, C, AluOpType.max, AluOpType.mult).then_inc(S.hr, 1)
-    g.vector.tensor_scalar(T.h[:, 3:4 * NC:4], T.z1[:, 0:NC], 0.0, -C, AluOpType.min, AluOpType.mult).then_inc(S.hr, 1)
-    g.vector.wait_ge(S.hr, 4)
-    g.vector.quantize_mx(T.E[:, D:D + NC], T.ES[:, D:D + NC], T.h[:]).then_inc(S.hq, 1)
+    za, zb = T.z1[:, z_first:z_first + D], T.z1[:, z_second:z_second + D]
+    g.vector.tensor_scalar(rows(2, h_first), za, 0.0, C, AluOpType.max, AluOpType.mult).then_inc(S.h1, 1)
+    g.vector.tensor_scalar(rows(3, h_first), za, 0.0, -C, AluOpType.min, AluOpType.mult).then_inc(S.h1, 1)
+    g.vector.wait_ge(S.h1, 4)
+    g.vector.quantize_mx(T.QF[:], T.SF[:], T.h[:, 4 * pack:4 * (pack + NC)]).then_inc(S.hf, 1)
+    g.scalar.wait_ge(S.h1, 4)
+    g.scalar.activation(rows(2, h_second), zb, relu, scale=C).then_inc(S.h2, 1)
+    g.scalar.activation(rows(3, h_second), zb, relu, scale=-C).then_inc(S.h2, 1)
+    g.vector.wait_ge(S.h2, 4)
+    g.vector.quantize_mx(T.E[:, D:D + NC], T.ES[:, D:D + NC], T.h[:, 4 * whole:4 * (whole + NC)]).then_inc(S.hq, 1)
 
     es = engines(topo.mask(core, prev) & topo.mask(core, nxt))
-    halves = (es[0::2], es[1::2])
+    to_prev = (prev, D + NC, S.from_next)
+    to_next = (nxt, 0, S.from_prev)
+    (dst1, at1, sem1), (dst2, at2, sem2) = (to_next, to_prev) if first_is_next else (to_prev, to_next)
+    rid1, pid1 = topo.addr(dst1, core)
+    rid2, pid2 = topo.addr(dst2, core)
+    mask1, mask2 = sum(es[0::2]), sum(es[1::2])
+    own2 = D + z_second
 
-    def halo(buf, cast):
-        out = []
-        for k, (dst, a, b, sem) in enumerate(((prev, D, D + NC, S.from_next), (nxt, NC, 0, S.from_prev))):
-            rid, pid = topo.addr(dst, core)
-            src, to = buf[:, a:a + D], buf[:, b:b + D]
-            if cast:
-                src, to = src.bitcast(dt.uint8), to.bitcast(dt.uint8)
-            out.append(RemoteDMATransfer(dst_ids=[DstId(rid=rid, pnc=pid)], dma_engine_mask=sum(halves[k]),
-                                         remote_sem=sem, src=src, dst=to))
-        return out
-
+    g.wait_ge(S.hf, 1)
+    g.remote_dma(T.E[:, at1:at1 + D].bitcast(dt.uint8), T.QF[:, qf:qf + D].bitcast(dt.uint8), sem1, S.sent, pid1, rid1, mask1)
     g.wait_ge(S.hq, 1)
-    g.remote_dma_fused(halo(T.E, True), local_sem=S.sent)
-    g.remote_dma_fused(halo(T.ES, False), local_sem=S.sent)
+    g.remote_dma(T.E[:, at2:at2 + D].bitcast(dt.uint8), T.E[:, own2:own2 + D].bitcast(dt.uint8), sem2, S.sent, pid2, rid2, mask2)
+    g.remote_dma_fused([
+        RemoteDMATransfer(dst_ids=[DstId(rid=rid1, pnc=pid1)], dma_engine_mask=mask1, remote_sem=sem1,
+                          src=T.SF[:, qf:qf + D], dst=T.ES[:, at1:at1 + D]),
+        RemoteDMATransfer(dst_ids=[DstId(rid=rid2, pnc=pid2)], dma_engine_mask=mask2, remote_sem=sem2,
+                          src=T.ES[:, own2:own2 + D], dst=T.ES[:, at2:at2 + D]),
+    ], local_sem=S.sent)
     g.wait_ge(S.sent, 2 * len(es))
 
     g.vector.wait_ge(S.ldt, 16)
@@ -94,10 +120,13 @@ def rank_program(g, core, T, topo):
     g.tensor.wait_ge(S.hq, 1)
     g.tensor.wait_ge(S.tq, 1)
     tap(1, True, False)
-    ends = [(0, prev, S.from_prev, len(halves[1])), (2, nxt, S.from_next, len(halves[0]))]
-    ends.sort(key=lambda e: topo.rack(topo.host(e[1])) != topo.rack(topo.host(core)))
-    for i, (t, _src, sem, cnt) in enumerate(ends):
-        g.tensor.wait_ge(sem, 2 * cnt)
+    turns = [(0, S.from_prev), (2, S.from_next)]
+    if first_is_next:
+        turns.reverse()
+    if topo.rack(topo.host(dst1)) != topo.rack(topo.host(core)):
+        turns.reverse()
+    for i, (t, sem) in enumerate(turns):
+        g.tensor.wait_ge(sem, len(es))
         tap(t, False, i == 1)
 
     g.vector.wait_ge(S.ysum, 3)

from concourse.bass import DstId, RemoteDMATransfer
from concourse.mybir import dt, AluOpType, ActivationFunctionType

NC, D = 128, 64
C = 0.023
NE = NC + 2 * D

SCRATCH = {
    "xs": ("sbuf", [128, 4 * NC], "bfloat16"),
    "w1s": ("sbuf", [128, 2 * 512], "bfloat16"),
    "wts": ("sbuf", [128, 3 * 512], "bfloat16"),
    "h": ("sbuf", [128, 4 * (NC + D)], "bfloat16"),
    "qx": ("sbuf", [128, NC], "float8_e4m3fn_x4"),
    "sx": ("sbuf", [128, NC], "uint8"),
    "qw": ("sbuf", [128, 2 * 128], "float8_e4m3fn_x4"),
    "sw": ("sbuf", [128, 2 * 128], "uint8"),
    "qt": ("sbuf", [128, 3 * 128], "float8_e4m3fn_x4"),
    "st": ("sbuf", [128, 3 * 128], "uint8"),
    "QF": ("sbuf", [128, NC], "float8_e4m3fn_x4"),
    "SF": ("sbuf", [128, NC], "uint8"),
    "E": ("sbuf", [128, NE], "float8_e4m3fn_x4"),
    "ES": ("sbuf", [128, NE], "uint8"),
    "ys": ("sbuf", [128, NC], "float32"),
    "z0": ("psum", [128, 512], "float32"),
    "z1": ("psum", [128, 512], "float32"),
    "yp": ("psum", [128, 512], "float32"),
}
SEMAPHORES = ["ldx", "ldw0", "ldw1", "ldt", "zero", "q0", "q1", "m0", "m1", "h1", "h2", "hf", "hq", "tq", "ysum", "ycp",
              "stored", "from_prev", "from_next", "sent"]


def engines(mask):
    return [1 << i for i in range(mask.bit_length()) if mask >> i & 1]


def rank_program(g, core, T, topo):
    r = T.rank_of(core)
    if r is None:
        return
    n = len(T.cores)
    prev, nxt = T.cores[(r - 1) % n], T.cores[(r + 1) % n]
    S = T.sem

    first_is_next = topo.host(nxt) != topo.host(core)
    z_first, z_second = (D, 0) if first_is_next else (0, D)
    h_first, h_second, h_zero = (D, 0, NC) if first_is_next else (D, NC, 0)
    pack = min(h_first, h_zero)
    whole = min(h_first, h_second)
    qf = h_first - pack

    g.sync.dma_start(T.xs[:], T.x[:]).then_inc(S.ldx, 16)
    g.scalar.dma_start(T.w1s[:, 0:512], T.w1[:, 0:512]).then_inc(S.ldw0, 16)
    g.sync.dma_start(T.w1s[:, 512:1024], T.w1[:, 512:1024]).then_inc(S.ldw1, 16)
    g.sync.wait_ge(S.ldw0, 16)
    g.sync.dma_start(T.wts[:], T.wt[:]).then_inc(S.ldt, 16)

    g.vector.memset(T.h[:, 4 * h_zero:4 * (h_zero + D)], 0.0).then_inc(S.zero, 1)
    g.vector.wait_ge(S.zero, 1)
    g.vector.wait_ge(S.ldx, 16)
    g.vector.quantize_mx(T.qx[:], T.sx[:], T.xs[:]).then_inc(S.q0, 1)
    g.vector.wait_ge(S.ldw0, 16)
    g.vector.quantize_mx(T.qw[:, 0:128], T.sw[:, 0:128], T.w1s[:, 0:512]).then_inc(S.q0, 1)
    g.vector.wait_ge(S.ldw1, 16)
    g.vector.quantize_mx(T.qw[:, 128:256], T.sw[:, 128:256], T.w1s[:, 512:1024]).then_inc(S.q1, 1)

    g.tensor.wait_ge(S.q0, 2)
    g.tensor.matmul_mx(T.z0[:, 0:NC], T.qw[:, 0:128], T.sw[:, 0:128], T.qx[:], T.sx[:], True, True).then_inc(S.m0, 1)
    g.tensor.wait_ge(S.q1, 1)
    g.tensor.matmul_mx(T.z1[:, 0:NC], T.qw[:, 128:256], T.sw[:, 128:256], T.qx[:], T.sx[:], True, True).then_inc(S.m1, 1)

    relu = ActivationFunctionType.Relu

    def rows(b, at):
        return T.h[:, 4 * at + b:4 * (at + D):4]

    g.scalar.wait_ge(S.m0, 1)
    for at, z, sem in ((h_first, z_first, S.h1), (h_second, z_second, S.h2)):
        g.scalar.activation(rows(0, at), T.z0[:, z:z + D], relu, scale=C).then_inc(sem, 1)
        g.scalar.activation(rows(1, at), T.z0[:, z:z + D], relu, scale=-C).then_inc(sem, 1)
    g.vector.wait_ge(S.m1, 1)
    za, zb = T.z1[:, z_first:z_first + D], T.z1[:, z_second:z_second + D]
    g.vector.tensor_scalar(rows(2, h_first), za, 0.0, C, AluOpType.max, AluOpType.mult).then_inc(S.h1, 1)
    g.vector.tensor_scalar(rows(3, h_first), za, 0.0, -C, AluOpType.min, AluOpType.mult).then_inc(S.h1, 1)
    g.vector.wait_ge(S.h1, 4)
    g.vector.quantize_mx(T.QF[:], T.SF[:], T.h[:, 4 * pack:4 * (pack + NC)]).then_inc(S.hf, 1)
    g.scalar.wait_ge(S.h1, 4)
    g.scalar.activation(rows(2, h_second), zb, relu, scale=C).then_inc(S.h2, 1)
    g.scalar.activation(rows(3, h_second), zb, relu, scale=-C).then_inc(S.h2, 1)
    g.vector.wait_ge(S.h2, 4)
    g.vector.quantize_mx(T.E[:, D:D + NC], T.ES[:, D:D + NC], T.h[:, 4 * whole:4 * (whole + NC)]).then_inc(S.hq, 1)

    es = engines(topo.mask(core, prev) & topo.mask(core, nxt))
    to_prev = (prev, D + NC, S.from_next)
    to_next = (nxt, 0, S.from_prev)
    (dst1, at1, sem1), (dst2, at2, sem2) = (to_next, to_prev) if first_is_next else (to_prev, to_next)
    rid1, pid1 = topo.addr(dst1, core)
    rid2, pid2 = topo.addr(dst2, core)
    mask1, mask2 = sum(es[0::2]), sum(es[1::2])
    own2 = D + z_second

    g.wait_ge(S.hf, 1)
    g.remote_dma(T.E[:, at1:at1 + D].bitcast(dt.uint8), T.QF[:, qf:qf + D].bitcast(dt.uint8), sem1, S.sent, pid1, rid1, mask1)
    g.wait_ge(S.hq, 1)
    g.remote_dma(T.E[:, at2:at2 + D].bitcast(dt.uint8), T.E[:, own2:own2 + D].bitcast(dt.uint8), sem2, S.sent, pid2, rid2, mask2)
    g.remote_dma_fused([
        RemoteDMATransfer(dst_ids=[DstId(rid=rid1, pnc=pid1)], dma_engine_mask=mask1, remote_sem=sem1,
                          src=T.SF[:, qf:qf + D], dst=T.ES[:, at1:at1 + D]),
        RemoteDMATransfer(dst_ids=[DstId(rid=rid2, pnc=pid2)], dma_engine_mask=mask2, remote_sem=sem2,
                          src=T.ES[:, own2:own2 + D], dst=T.ES[:, at2:at2 + D]),
    ], local_sem=S.sent)
    g.wait_ge(S.sent, 2 * len(es))

    g.vector.wait_ge(S.ldt, 16)
    g.vector.quantize_mx(T.qt[:], T.st[:], T.wts[:]).then_inc(S.tq, 1)

    def tap(t, start, stop):
        g.tensor.matmul_mx(T.yp[:, 0:NC], T.qt[:, 128 * t:128 * t + 128], T.st[:, 128 * t:128 * t + 128],
                           T.E[:, D * t:D * t + NC], T.ES[:, D * t:D * t + NC], start, stop).then_inc(S.ysum, 1)

    g.tensor.wait_ge(S.hq, 1)
    g.tensor.wait_ge(S.tq, 1)
    tap(1, True, False)
    turns = [(0, S.from_prev), (2, S.from_next)]
    if first_is_next:
        turns.reverse()
    if topo.rack(topo.host(dst1)) != topo.rack(topo.host(core)):
        turns.reverse()
    for i, (t, sem) in enumerate(turns):
        g.tensor.wait_ge(sem, len(es))
        tap(t, False, i == 1)

    g.vector.wait_ge(S.ysum, 3)
    g.vector.tensor_copy(T.ys[:], T.yp[:, 0:NC]).then_inc(S.ycp, 1)
    g.sync.wait_ge(S.ycp, 1)
    g.sync.dma_start(T.y[:], T.ys[:]).then_inc(S.stored, 16)
    g.sync.wait_ge(S.stored, 16)
